import numpy as np
import ml_dtypes

BF16 = ml_dtypes.bfloat16


def bf(x):
    return np.asarray(x, np.float32).astype(BF16)


def f32(x):
    return np.asarray(x, np.float32)


def f64(x):
    return np.asarray(x).astype(np.float64)


def striped(idx):
    return np.tile(idx.reshape(-1, 16).T, (8, 1))


def rows(idx, k):
    return np.tile(idx, (k, 1))


def look(tab, idx):
    return np.take_along_axis(f64(tab), rows(idx, len(tab)), axis=1)


K, S, V, N, M = 256, 2048, 512, 512, 128


def setup_inputs():
    return {"tab": f32(np.random.standard_normal((2, K, S))), "y": f32(np.random.standard_normal((K, V))), "w": bf(np.random.standard_normal((K, M)) / np.sqrt(K)), "b": f32(0.5 * np.random.standard_normal((M, 1))), "offs": striped(np.random.permutation(S)[:N])}


def reference(tab, y, w, b, offs):
    idx = offs[:16].T.reshape(-1)
    x = (np.maximum(look(tab[0], idx), f64(y))) * (1.0 / (1.0 + np.exp(-look(tab[1], idx))))
    return np.maximum(f64(w).T @ x + f64(b), 0.0)

@@ -1,0 +1,42 @@
+import concourse.mybir as mybir
+
+F32, BF16, U16 = mybir.dt.float32, mybir.dt.bfloat16, mybir.dt.uint16
+ALU, ACT = mybir.AluOpType, mybir.ActivationFunctionType
+
+P = 128
+K, S, N, M = 256, 2048, 512, 128
+BLOCKS = K // P
+FLOPS = 2 * K * M * N
+
+
+def tile_lookup_vg_maxsig_relu_kernel(tc, tab, y, w, b, offs, out):
+    nc = tc.nc
+    with (
+        tc.tile_pool(name="sbuf", bufs=1) as sbuf,
+        tc.psum_pool(name="psum", bufs=1) as psum,
+    ):
+        offsets = sbuf.tile([P, N // 16], U16, name="offsets")
+        nc.sync.dma_start(offsets[:], offs)
+        bias = sbuf.tile([M, 1], F32, name="bias")
+        nc.sync.dma_start(bias[:], b)
+        acc = psum.tile([M, N], F32, name="acc")
+        for k in range(BLOCKS):
+            rows = slice(k * P, (k + 1) * P)
+            values = sbuf.tile([P, S], F32, name=f"values{k}")
+            gates = sbuf.tile([P, S], F32, name=f"gates{k}")
+            stream = sbuf.tile([P, N], F32, name=f"stream{k}")
+            weights = sbuf.tile([P, M], BF16, name=f"weights{k}")
+            nc.sync.dma_start(weights[:], w[rows, :])
+            nc.sync.dma_start(stream[:], y[rows, :])
+            nc.sync.dma_start(values[:], tab[0, rows, :])
+            nc.sync.dma_start(gates[:], tab[1, rows, :])
+            larger = sbuf.tile([P, N], F32, name=f"larger{k}")
+            opened = sbuf.tile([P, N], F32, name=f"opened{k}")
+            x = sbuf.tile([P, N], BF16, name=f"x{k}")
+            nc.vector.tensor_tensor(larger[:], values[:].indirect(offsets[:]), stream[:], ALU.max)
+            nc.scalar.activation(opened[:], gates[:].indirect(offsets[:]), ACT.Sigmoid)
+            nc.vector.tensor_tensor(x[:], larger[:], opened[:], ALU.mult)
+            nc.tensor.matmul(acc[:], weights[:], x[:], start=(k == 0), stop=(k == BLOCKS - 1))
+        result = sbuf.tile([M, N], F32, name="result")
+        nc.scalar.activation(result[:], acc[:], ACT.Relu, bias=bias[:])
+        nc.sync.dma_start(out, result[:])

@@ -6,37 +6,52 @@ ALU, ACT = mybir.AluOpType, mybir.ActivationFunctionType
 P = 128
 K, S, N, M = 256, 2048, 512, 128
 BLOCKS = K // P
+PIECES = 4
+WIDTH = N // PIECES
 FLOPS = 2 * K * M * N
 
 
 def tile_lookup_vg_maxsig_relu_kernel(tc, tab, y, w, b, offs, out):
     nc = tc.nc
+    tab_blocks = tab.rearrange("t (p k) s -> t k p s", k=BLOCKS)
     with (
         tc.tile_pool(name="sbuf", bufs=1) as sbuf,
         tc.psum_pool(name="psum", bufs=1) as psum,
     ):
+        values = [sbuf.tile([P, S], F32, name=f"values{k}") for k in range(BLOCKS)]
+        gates = [sbuf.tile([P, S], F32, name=f"gates{k}") for k in range(BLOCKS)]
         offsets = sbuf.tile([P, N // 16], U16, name="offsets")
-        nc.sync.dma_start(offsets[:], offs)
+        stream = sbuf.tile([P, BLOCKS * N], F32, name="stream")
+        weights = sbuf.tile([P, BLOCKS * M], BF16, name="weights")
         bias = sbuf.tile([M, 1], F32, name="bias")
-        nc.sync.dma_start(bias[:], b)
-        acc = psum.tile([M, N], F32, name="acc")
+
+        nc.sync.dma_start(values[0][:], tab_blocks[0, 0])
+        nc.sync.dma_start(offsets[:], offs)
+        nc.sync.dma_start(stream[:], y.rearrange("(p k) n -> p (k n)", k=BLOCKS))
+        nc.sync.dma_start(weights[:], w.rearrange("(p k) m -> p (k m)", k=BLOCKS))
+        nc.sync.dma_start(gates[0][:], tab_blocks[1, 0])
+        nc.sync.dma_start(values[1][:], tab_blocks[0, 1])
+        nc.sync.dma_start(gates[1][:], tab_blocks[1, 1])
+        nc.scalar.dma_start(bias[:], b)
+
+        acc = [psum.tile([M, WIDTH], F32, name=f"acc{i}") for i in range(PIECES)]
+        result = sbuf.tile([M, N], F32, name="result")
         for k in range(BLOCKS):
-            rows = slice(k * P, (k + 1) * P)
-            values = sbuf.tile([P, S], F32, name=f"values{k}")
-            gates = sbuf.tile([P, S], F32, name=f"gates{k}")
-            stream = sbuf.tile([P, N], F32, name=f"stream{k}")
-            weights = sbuf.tile([P, M], BF16, name=f"weights{k}")
-            nc.sync.dma_start(weights[:], w[rows, :])
-            nc.sync.dma_start(stream[:], y[rows, :])
-            nc.sync.dma_start(values[:], tab[0, rows, :])
-            nc.sync.dma_start(gates[:], tab[1, rows, :])
             larger = sbuf.tile([P, N], F32, name=f"larger{k}")
             opened = sbuf.tile([P, N], F32, name=f"opened{k}")
             x = sbuf.tile([P, N], BF16, name=f"x{k}")
-            nc.vector.tensor_tensor(larger[:], values[:].indirect(offsets[:]), stream[:], ALU.max)
-            nc.scalar.activation(opened[:], gates[:].indirect(offsets[:]), ACT.Sigmoid)
-            nc.vector.tensor_tensor(x[:], larger[:], opened[:], ALU.mult)
-            nc.tensor.matmul(acc[:], weights[:], x[:], start=(k == 0), stop=(k == BLOCKS - 1))
-        result = sbuf.tile([M, N], F32, name="result")
-        nc.scalar.activation(result[:], acc[:], ACT.Relu, bias=bias[:])
-        nc.sync.dma_start(out, result[:])
+            nc.vector.tensor_tensor(
+                larger[:], values[k][:].indirect(offsets[:]), stream[:, k * N : (k + 1) * N], ALU.max
+            )
+            for i in range(PIECES):
+                cols = slice(i * WIDTH, (i + 1) * WIDTH)
+                piece = offsets[:, i * WIDTH // 16 : (i + 1) * WIDTH // 16]
+                nc.scalar.activation(opened[:, cols], gates[k][:].indirect(piece), ACT.Sigmoid)
+                nc.vector.tensor_tensor(x[:, cols], larger[:, cols], opened[:, cols], ALU.mult)
+                nc.tensor.matmul(
+                    acc[i][:], weights[:, k * M : (k + 1) * M], x[:, cols], start=(k == 0), stop=(k == BLOCKS - 1)
+                )
+        for i in range(PIECES):
+            cols = slice(i * WIDTH, (i + 1) * WIDTH)
+            nc.vector.tensor_scalar(result[:, cols], acc[i][:], bias[:], 0.0, ALU.add, ALU.max)
+            nc.sync.dma_start(out[:, cols], result[:, cols])

@@ -25,14 +25,14 @@ def tile_lookup_vg_maxsig_relu_kernel(tc, tab, y, w, b, offs, out):
         weights = sbuf.tile([P, BLOCKS * M], BF16, name="weights")
         bias = sbuf.tile([M, 1], F32, name="bias")
 
-        nc.sync.dma_start(values[0][:], tab_blocks[0, 0])
+        nc.scalar.dma_start(values[0][:], tab_blocks[0, 0])
         nc.sync.dma_start(offsets[:], offs)
         nc.sync.dma_start(stream[:], y.rearrange("(p k) n -> p (k n)", k=BLOCKS))
-        nc.sync.dma_start(weights[:], w.rearrange("(p k) m -> p (k m)", k=BLOCKS))
         nc.sync.dma_start(gates[0][:], tab_blocks[1, 0])
         nc.sync.dma_start(values[1][:], tab_blocks[0, 1])
         nc.sync.dma_start(gates[1][:], tab_blocks[1, 1])
-        nc.scalar.dma_start(bias[:], b)
+        nc.sync.dma_start(weights[:], w.rearrange("(p k) m -> p (k m)", k=BLOCKS))
+        nc.sync.dma_start(bias[:], b)
 
         acc = [psum.tile([M, WIDTH], F32, name=f"acc{i}") for i in range(PIECES)]
         result = sbuf.tile([M, N], F32, name="result")
@@ -53,5 +53,5 @@ def tile_lookup_vg_maxsig_relu_kernel(tc, tab, y, w, b, offs, out):
                 )
         for i in range(PIECES):
             cols = slice(i * WIDTH, (i + 1) * WIDTH)
-            nc.vector.tensor_scalar(result[:, cols], acc[i][:], bias[:], 0.0, ALU.add, ALU.max)
+            nc.scalar.activation(result[:, cols], acc[i][:], ACT.Relu, bias=bias[:])
             nc.sync.dma_start(out[:, cols], result[:, cols])

@@ -25,11 +25,11 @@ def tile_lookup_vg_maxsig_relu_kernel(tc, tab, y, w, b, offs, out):
         weights = sbuf.tile([P, BLOCKS * M], BF16, name="weights")
         bias = sbuf.tile([M, 1], F32, name="bias")
 
-        nc.scalar.dma_start(values[0][:], tab_blocks[0, 0])
+        for k in range(BLOCKS):
+            nc.scalar.dma_start(values[k][:], tab_blocks[0, k])
         nc.sync.dma_start(offsets[:], offs)
-        nc.sync.dma_start(stream[:], y.rearrange("(p k) n -> p (k n)", k=BLOCKS))
         nc.sync.dma_start(gates[0][:], tab_blocks[1, 0])
-        nc.sync.dma_start(values[1][:], tab_blocks[0, 1])
+        nc.sync.dma_start(stream[:], y.rearrange("(p k) n -> p (k n)", k=BLOCKS))
         nc.sync.dma_start(gates[1][:], tab_blocks[1, 1])
         nc.sync.dma_start(weights[:], w.rearrange("(p k) m -> p (k m)", k=BLOCKS))
         nc.sync.dma_start(bias[:], b)

import concourse.mybir as mybir

F32, BF16, U16 = mybir.dt.float32, mybir.dt.bfloat16, mybir.dt.uint16
ALU, ACT = mybir.AluOpType, mybir.ActivationFunctionType

P = 128
K, S, N, M = 256, 2048, 512, 128
BLOCKS = K // P
PIECES = 4
WIDTH = N // PIECES
FLOPS = 2 * K * M * N


def tile_lookup_vg_maxsig_relu_kernel(tc, tab, y, w, b, offs, out):
    nc = tc.nc
    tab_blocks = tab.rearrange("t (p k) s -> t k p s", k=BLOCKS)
    with (
        tc.tile_pool(name="sbuf", bufs=1) as sbuf,
        tc.psum_pool(name="psum", bufs=1) as psum,
    ):
        values = [sbuf.tile([P, S], F32, name=f"values{k}") for k in range(BLOCKS)]
        gates = [sbuf.tile([P, S], F32, name=f"gates{k}") for k in range(BLOCKS)]
        offsets = sbuf.tile([P, N // 16], U16, name="offsets")
        stream = sbuf.tile([P, BLOCKS * N], F32, name="stream")
        weights = sbuf.tile([P, BLOCKS * M], BF16, name="weights")
        bias = sbuf.tile([M, 1], F32, name="bias")

        for k in range(BLOCKS):
            nc.scalar.dma_start(values[k][:], tab_blocks[0, k])
        nc.sync.dma_start(offsets[:], offs)
        nc.sync.dma_start(gates[0][:], tab_blocks[1, 0])
        nc.sync.dma_start(stream[:], y.rearrange("(p k) n -> p (k n)", k=BLOCKS))
        nc.sync.dma_start(gates[1][:], tab_blocks[1, 1])
        nc.sync.dma_start(weights[:], w.rearrange("(p k) m -> p (k m)", k=BLOCKS))
        nc.sync.dma_start(bias[:], b)

        acc = [psum.tile([M, WIDTH], F32, name=f"acc{i}") for i in range(PIECES)]
        result = sbuf.tile([M, N], F32, name="result")
        for k in range(BLOCKS):
            larger = sbuf.tile([P, N], F32, name=f"larger{k}")
            opened = sbuf.tile([P, N], F32, name=f"opened{k}")
            x = sbuf.tile([P, N], BF16, name=f"x{k}")
            nc.vector.tensor_tensor(
                larger[:], values[k][:].indirect(offsets[:]), stream[:, k * N : (k + 1) * N], ALU.max
            )
            for i in range(PIECES):
                cols = slice(i * WIDTH, (i + 1) * WIDTH)
                piece = offsets[:, i * WIDTH // 16 : (i + 1) * WIDTH // 16]
                nc.scalar.activation(opened[:, cols], gates[k][:].indirect(piece), ACT.Sigmoid)
                nc.vector.tensor_tensor(x[:, cols], larger[:, cols], opened[:, cols], ALU.mult)
                nc.tensor.matmul(
                    acc[i][:], weights[:, k * M : (k + 1) * M], x[:, cols], start=(k == 0), stop=(k == BLOCKS - 1)
                )
        for i in range(PIECES):
            cols = slice(i * WIDTH, (i + 1) * WIDTH)
            nc.scalar.activation(result[:, cols], acc[i][:], ACT.Relu, bias=bias[:])
            nc.sync.dma_start(out[:, cols], result[:, cols])
